import numpy as np, ml_dtypes
CORES = [9,17,57,81,121,137,145,185,209,249]
N = 10
KT, C = 2, 64
def setup_inputs(rng):
    return {"x": rng.standard_normal((N, 128, KT * C), dtype=np.float32).astype(ml_dtypes.bfloat16)}
def setup_inputs_big(rng):
    d = setup_inputs(rng)
    for k in ("x",): d[k] = (d[k].astype(np.float32) * 1024.0).astype(d[k].dtype)
    return d
def setup_inputs_small(rng):
    d = setup_inputs(rng)
    for k in ("x",): d[k] = (d[k].astype(np.float32) * (1 / 1024.0)).astype(d[k].dtype)
    return d
def setup_inputs_apart(rng):
    d = setup_inputs(rng)
    f = (10.0 ** rng.permutation(np.linspace(-1.5, 1.5, N))).astype(np.float32).reshape(N, 1, 1)
    for k in ("x",): d[k] = (d[k].astype(np.float32) * f).astype(d[k].dtype)
    return d
def reference(x):
    X = x.astype(np.float64)
    y = np.full((N, C, N * C), np.nan)
    for r in range(N):
        for i in range(N):
            s = i
            if s != r: y[r][:, C * i:C * i + C] = sum(X[r][:, C * t:C * t + C].T @ X[s][:, C * t:C * t + C] for t in range(KT))
    return {"y": y.astype(ml_dtypes.bfloat16 if x.dtype != np.float64 else np.float64)}

@@ -1,0 +1,153 @@
+from concourse.bass import DstId, RemoteDMATransfer
+
+N, KT, C = 10, 2, 64
+W = KT * C
+BANKS = 8
+DIRECT = 3
+
+SCRATCH = {
+    "stage": ("dram", [128, W], "bfloat16"),
+    "land": ("sbuf", [128, N * W], "bfloat16"),
+    "ysb": ("sbuf", [128, N * C], "bfloat16"),
+}
+for _b in range(BANKS):
+    SCRATCH["ps%d" % _b] = ("psum", [128, 512], "float32")
+
+SEMAPHORES = (["ld_stage", "ld_land", "handed", "sent", "copied", "stored"]
+              + ["arr%d" % _s for _s in range(N)] + ["mm%d" % _b for _b in range(BANKS)])
+
+
+def _count(mask):
+    return bin(mask).count("1")
+
+
+def _plan(cores, topo):
+    n = len(cores)
+    world = range((max(topo.host(c) for c in cores) + 1) * topo.CORES_PER_HOST)
+    plan = []
+    for i, c in enumerate(cores):
+        same = [j for j in range(n) if j != i and topo.may_write(c, cores[j])]
+        cross = [j for j in range(n) if j != i and not topo.may_write(c, cores[j])]
+        peers = sorted(same + [i])
+        p = peers.index(i)
+        ring = peers[p + 1:] + peers[:p]
+        chip = [k for k in world if k != c and topo.host(k) == topo.host(c) and topo.chip(k) == topo.chip(c)]
+        ports = [k for k in chip if all(topo.may_write(k, cores[j]) for j in cross)]
+        plain = [k for k in chip if k not in ports]
+        dies = sorted({topo.die(k) for k in ports})
+        load = {k: [] for k in ports}
+        for q, j in enumerate(cross):
+            d = dies[(p + q) % len(dies)]
+            k = min([k for k in ports if topo.die(k) == d], key=lambda k: (len(load[k]), k))
+            load[k].append(j)
+        pool = {d: [k for k in plain if topo.die(k) == d] for d in sorted({topo.die(k) for k in plain})}
+        helpers = []
+        while any(pool.values()):
+            for d in pool:
+                if pool[d]:
+                    helpers.append(pool[d].pop(0))
+        direct, rest = ring[:DIRECT], ring[DIRECT:]
+        for j, k in zip(rest, helpers):
+            load[k] = [j]
+        direct = direct + rest[len(helpers):]
+        relays = sorted([(k, v) for k, v in load.items() if v], key=lambda kv: (-len(kv[1]), kv[0] in plain, kv[0]))
+        plan.append((direct, relays))
+    return plan
+
+
+def _write(g, T, topo, core, dsts, src, out, sem, mask):
+    ids = []
+    for d in dsts:
+        rid, pid = topo.addr(d, core)
+        ids.append(DstId(rid=rid, pnc=pid))
+    g.remote_dma_fused([RemoteDMATransfer(dst_ids=ids, dma_engine_mask=mask, remote_sem=sem, srcs=[src],
+                                          dsts=[out for _ in dsts], alu_op=0)], local_sem=T.sem.sent)
+    return _count(mask)
+
+
+def _common_mask(topo, core, dsts):
+    m = topo.mask(core, dsts[0])
+    for d in dsts[1:]:
+        m &= topo.mask(core, d)
+    return m
+
+
+def rank_program(g, core, T, topo):
+    cores = list(T.cores)
+    plan = _plan(cores, topo)
+    rank = T.rank_of(core)
+
+    if rank is None:
+        for i, (direct, relays) in enumerate(plan):
+            for k, ranks in relays:
+                if k != core:
+                    continue
+                hand = _hand_mask(topo, cores, i, plan)
+                g.wait_ge(T.sem.handed, _count(hand))
+                dsts = [cores[j] for j in ranks]
+                sent = _write(g, T, topo, core, dsts, T.stage[:, :], T.land[:, i * W:(i + 1) * W],
+                              T.sem["arr%d" % i], _common_mask(topo, core, dsts))
+                g.wait_ge(T.sem.sent, sent)
+        return
+
+    direct, relays = plan[rank]
+    own = T.land[:, rank * W:(rank + 1) * W]
+
+    g.sync.dma_start(T.stage[:, :], T.x[:, :]).then_inc(T.sem.ld_stage, 16)
+    g.scalar.dma_start(own, T.x[:, :]).then_inc(T.sem.ld_land, 16)
+    g.vector.memset(T.ysb[0:C, rank * C:(rank + 1) * C], 0.0).then_inc(T.sem.copied, 1)
+
+    g.wait_ge(T.sem.ld_stage, 16)
+    sent = 0
+    if relays:
+        sent += _write(g, T, topo, core, [k for k, _ in relays], T.stage[:, :], T.stage[:, :], T.sem.handed,
+                       _hand_mask(topo, cores, rank, plan))
+    if direct:
+        dsts = [cores[j] for j in direct]
+        sent += _write(g, T, topo, core, dsts, T.stage[:, :], own, T.sem["arr%d" % rank],
+                       _common_mask(topo, core, dsts))
+
+    expect = []
+    for i, (d_i, r_i) in enumerate(plan):
+        if rank in d_i:
+            m = _common_mask(topo, cores[i], [cores[j] for j in d_i])
+            expect.append(((0, d_i.index(rank), 0), i, _count(m)))
+        for pos, (k, ranks) in enumerate(r_i):
+            if rank in ranks:
+                m = _common_mask(topo, k, [cores[j] for j in ranks])
+                expect.append(((1, ranks.index(rank), pos), i, _count(m)))
+    expect.sort()
+    jobs = [[e] for e in expect]
+    while len(jobs) > BANKS:
+        jobs = [jobs[0] + jobs[1]] + jobs[2:]
+
+    g.tensor.wait_ge(T.sem.ld_land, 16)
+    for b, job in enumerate(jobs):
+        for n_in_job, (_, s, inc) in enumerate(job):
+            g.tensor.wait_ge(T.sem["arr%d" % s], inc)
+            out = T["ps%d" % b][0:C, n_in_job * C:(n_in_job + 1) * C]
+            for t in range(KT):
+                mm = g.tensor.matmul(out, T.land[:, rank * W + t * C:rank * W + (t + 1) * C],
+                                     T.land[:, s * W + t * C:s * W + (t + 1) * C], t == 0, t == KT - 1)
+            mm.then_inc(T.sem["mm%d" % b], 1)
+
+    for b, job in enumerate(jobs):
+        g.vector.wait_ge(T.sem["mm%d" % b], len(job))
+        for n_in_job, (_, s, inc) in enumerate(job):
+            g.vector.tensor_copy(T.ysb[0:C, s * C:(s + 1) * C],
+                                 T["ps%d" % b][0:C, n_in_job * C:(n_in_job + 1) * C]).then_inc(T.sem.copied, 1)
+
+    g.sync.wait_ge(T.sem.copied, N)
+    g.sync.dma_start(T.y[:, :], T.ysb[0:C, :]).then_inc(T.sem.stored, 16)
+    g.sync.wait_ge(T.sem.stored, 16)
+    g.wait_ge(T.sem.sent, sent)
+
+
+def _hand_mask(topo, cores, i, plan):
+    direct, relays = plan[i]
+    on = _common_mask(topo, cores[i], [k for k, _ in relays])
+    if direct:
+        spare = on & ~_common_mask(topo, cores[i], [cores[j] for j in direct])
+        if spare:
+            return spare
+    return on

@@ -3,7 +3,6 @@ from concourse.bass import DstId, RemoteDMATransfer
 N, KT, C = 10, 2, 64
 W = KT * C
 BANKS = 8
-DIRECT = 3
 
 SCRATCH = {
     "stage": ("dram", [128, W], "bfloat16"),
@@ -13,8 +12,9 @@ SCRATCH = {
 for _b in range(BANKS):
     SCRATCH["ps%d" % _b] = ("psum", [128, 512], "float32")
 
-SEMAPHORES = (["ld_stage", "ld_land", "handed", "sent", "copied", "stored"]
-              + ["arr%d" % _s for _s in range(N)] + ["mm%d" % _b for _b in range(BANKS)])
+SEMAPHORES = (["ld_stage", "ld_land", "handed", "sent", "st0", "st1"]
+              + ["arr%d" % _s for _s in range(N)] + ["mm%d" % _b for _b in range(BANKS)]
+              + ["cp%d" % _b for _b in range(BANKS)])
 
 
 def _count(mask):
@@ -33,25 +33,25 @@ def _plan(cores, topo):
         ring = peers[p + 1:] + peers[:p]
         chip = [k for k in world if k != c and topo.host(k) == topo.host(c) and topo.chip(k) == topo.chip(c)]
         ports = [k for k in chip if all(topo.may_write(k, cores[j]) for j in cross)]
-        plain = [k for k in chip if k not in ports]
-        dies = sorted({topo.die(k) for k in ports})
-        load = {k: [] for k in ports}
-        for q, j in enumerate(cross):
-            d = dies[(p + q) % len(dies)]
-            k = min([k for k in ports if topo.die(k) == d], key=lambda k: (len(load[k]), k))
-            load[k].append(j)
-        pool = {d: [k for k in plain if topo.die(k) == d] for d in sorted({topo.die(k) for k in plain})}
-        helpers = []
-        while any(pool.values()):
-            for d in pool:
-                if pool[d]:
-                    helpers.append(pool[d].pop(0))
-        direct, rest = ring[:DIRECT], ring[DIRECT:]
-        for j, k in zip(rest, helpers):
-            load[k] = [j]
-        direct = direct + rest[len(helpers):]
-        relays = sorted([(k, v) for k, v in load.items() if v], key=lambda kv: (-len(kv[1]), kv[0] in plain, kv[0]))
-        plan.append((direct, relays))
+        dies = sorted({topo.die(k) for k in ports}, key=lambda d: (d != topo.die(c), d))
+        nd = len(dies)
+        by = {d: [k for k in ports if topo.die(k) == d] for d in dies}
+        npos, nc = len(ports), len(cross)
+        upper = 1 if 2 * p >= len(peers) else 0
+        load = [[] for _ in range(npos)]
+        if nc <= npos:
+            line = [by[dies[(k - p + upper) % nd]][k // nd] for k in range(npos)]
+            for slot in range(nc):
+                load[slot].append(cross[(slot - p) % nc])
+        else:
+            line = [by[d][0] for d in dies] + [by[dies[(a + p) % nd]][b] for b in range(1, npos // nd) for a in range(nd)]
+            two = nc - npos
+            early, rest = cross[:2 * two], cross[2 * two:]
+            for t in range(2 * two):
+                load[t % two].append(early[(t - p) % len(early)])
+            for u in range(len(rest)):
+                load[two + u].append(rest[(u + upper) % len(rest)])
+        plan.append((ring, [(k, v) for k, v in zip(line, load) if v]))
     return plan
 
 
@@ -72,6 +72,16 @@ def _common_mask(topo, core, dsts):
     return m
 
 
+def _hand_mask(topo, cores, i, plan):
+    direct, relays = plan[i]
+    on = _common_mask(topo, cores[i], [k for k, _ in relays])
+    if direct:
+        spare = on & ~_common_mask(topo, cores[i], [cores[j] for j in direct])
+        if spare:
+            return spare
+    return on
+
+
 def rank_program(g, core, T, topo):
     cores = list(T.cores)
     plan = _plan(cores, topo)
@@ -82,8 +92,7 @@ def rank_program(g, core, T, topo):
             for k, ranks in relays:
                 if k != core:
                     continue
-                hand = _hand_mask(topo, cores, i, plan)
-                g.wait_ge(T.sem.handed, _count(hand))
+                g.wait_ge(T.sem.handed, _count(_hand_mask(topo, cores, i, plan)))
                 dsts = [cores[j] for j in ranks]
                 sent = _write(g, T, topo, core, dsts, T.stage[:, :], T.land[:, i * W:(i + 1) * W],
                               T.sem["arr%d" % i], _common_mask(topo, core, dsts))
@@ -94,8 +103,7 @@ def rank_program(g, core, T, topo):
     own = T.land[:, rank * W:(rank + 1) * W]
 
     g.sync.dma_start(T.stage[:, :], T.x[:, :]).then_inc(T.sem.ld_stage, 16)
-    g.scalar.dma_start(own, T.x[:, :]).then_inc(T.sem.ld_land, 16)
-    g.vector.memset(T.ysb[0:C, rank * C:(rank + 1) * C], 0.0).then_inc(T.sem.copied, 1)
+    g.sync.dma_start(own, T.x[:, :]).then_inc(T.sem.ld_land, 16)
 
     g.wait_ge(T.sem.ld_stage, 16)
     sent = 0
@@ -135,19 +143,16 @@ def rank_program(g, core, T, topo):
         g.vector.wait_ge(T.sem["mm%d" % b], len(job))
         for n_in_job, (_, s, inc) in enumerate(job):
             g.vector.tensor_copy(T.ysb[0:C, s * C:(s + 1) * C],
-                                 T["ps%d" % b][0:C, n_in_job * C:(n_in_job + 1) * C]).then_inc(T.sem.copied, 1)
+                                 T["ps%d" % b][0:C, n_in_job * C:(n_in_job + 1) * C]).then_inc(T.sem["cp%d" % b], 1)
 
-    g.sync.wait_ge(T.sem.copied, N)
-    g.sync.dma_start(T.y[:, :], T.ysb[0:C, :]).then_inc(T.sem.stored, 16)
-    g.sync.wait_ge(T.sem.stored, 16)
+    queues = [g.sync, g.scalar]
+    stored = [0, 0]
+    for b, job in enumerate(jobs):
+        w = b % 2
+        queues[w].wait_ge(T.sem["cp%d" % b], len(job))
+        for _, s, inc in job:
+            queues[w].dma_start(T.y[:, s * C:(s + 1) * C], T.ysb[0:C, s * C:(s + 1) * C]).then_inc(T.sem["st%d" % w], 16)
+            stored[w] += 16
+    for w in range(2):
+        queues[w].wait_ge(T.sem["st%d" % w], stored[w])
     g.wait_ge(T.sem.sent, sent)
-
-
-def _hand_mask(topo, cores, i, plan):
-    direct, relays = plan[i]
-    on = _common_mask(topo, cores[i], [k for k, _ in relays])
-    if direct:
-        spare = on & ~_common_mask(topo, cores[i], [cores[j] for j in direct])
-        if spare:
-            return spare
-    return on

from concourse.bass import DstId, RemoteDMATransfer

N, KT, C = 10, 2, 64
W = KT * C
BANKS = 8

SCRATCH = {
    "stage": ("dram", [128, W], "bfloat16"),
    "land": ("sbuf", [128, N * W], "bfloat16"),
    "ysb": ("sbuf", [128, N * C], "bfloat16"),
}
for _b in range(BANKS):
    SCRATCH["ps%d" % _b] = ("psum", [128, 512], "float32")

SEMAPHORES = (["ld_stage", "ld_land", "handed", "sent", "st0", "st1"]
              + ["arr%d" % _s for _s in range(N)] + ["mm%d" % _b for _b in range(BANKS)]
              + ["cp%d" % _b for _b in range(BANKS)])


def _count(mask):
    return bin(mask).count("1")


def _plan(cores, topo):
    n = len(cores)
    world = range((max(topo.host(c) for c in cores) + 1) * topo.CORES_PER_HOST)
    plan = []
    for i, c in enumerate(cores):
        same = [j for j in range(n) if j != i and topo.may_write(c, cores[j])]
        cross = [j for j in range(n) if j != i and not topo.may_write(c, cores[j])]
        peers = sorted(same + [i])
        p = peers.index(i)
        ring = peers[p + 1:] + peers[:p]
        chip = [k for k in world if k != c and topo.host(k) == topo.host(c) and topo.chip(k) == topo.chip(c)]
        ports = [k for k in chip if all(topo.may_write(k, cores[j]) for j in cross)]
        dies = sorted({topo.die(k) for k in ports}, key=lambda d: (d != topo.die(c), d))
        nd = len(dies)
        by = {d: [k for k in ports if topo.die(k) == d] for d in dies}
        npos, nc = len(ports), len(cross)
        upper = 1 if 2 * p >= len(peers) else 0
        load = [[] for _ in range(npos)]
        if nc <= npos:
            line = [by[dies[(k - p + upper) % nd]][k // nd] for k in range(npos)]
            for slot in range(nc):
                load[slot].append(cross[(slot - p) % nc])
        else:
            line = [by[d][0] for d in dies] + [by[dies[(a + p) % nd]][b] for b in range(1, npos // nd) for a in range(nd)]
            two = nc - npos
            early, rest = cross[:2 * two], cross[2 * two:]
            for t in range(2 * two):
                load[t % two].append(early[(t - p) % len(early)])
            for u in range(len(rest)):
                load[two + u].append(rest[(u + upper) % len(rest)])
        plan.append((ring, [(k, v) for k, v in zip(line, load) if v]))
    return plan


def _write(g, T, topo, core, dsts, src, out, sem, mask):
    ids = []
    for d in dsts:
        rid, pid = topo.addr(d, core)
        ids.append(DstId(rid=rid, pnc=pid))
    g.remote_dma_fused([RemoteDMATransfer(dst_ids=ids, dma_engine_mask=mask, remote_sem=sem, srcs=[src],
                                          dsts=[out for _ in dsts], alu_op=0)], local_sem=T.sem.sent)
    return _count(mask)


def _common_mask(topo, core, dsts):
    m = topo.mask(core, dsts[0])
    for d in dsts[1:]:
        m &= topo.mask(core, d)
    return m


def _hand_mask(topo, cores, i, plan):
    direct, relays = plan[i]
    on = _common_mask(topo, cores[i], [k for k, _ in relays])
    if direct:
        spare = on & ~_common_mask(topo, cores[i], [cores[j] for j in direct])
        if spare:
            return spare
    return on


def rank_program(g, core, T, topo):
    cores = list(T.cores)
    plan = _plan(cores, topo)
    rank = T.rank_of(core)

    if rank is None:
        for i, (direct, relays) in enumerate(plan):
            for k, ranks in relays:
                if k != core:
                    continue
                g.wait_ge(T.sem.handed, _count(_hand_mask(topo, cores, i, plan)))
                dsts = [cores[j] for j in ranks]
                sent = _write(g, T, topo, core, dsts, T.stage[:, :], T.land[:, i * W:(i + 1) * W],
                              T.sem["arr%d" % i], _common_mask(topo, core, dsts))
                g.wait_ge(T.sem.sent, sent)
        return

    direct, relays = plan[rank]
    own = T.land[:, rank * W:(rank + 1) * W]

    g.sync.dma_start(T.stage[:, :], T.x[:, :]).then_inc(T.sem.ld_stage, 16)
    g.sync.dma_start(own, T.x[:, :]).then_inc(T.sem.ld_land, 16)

    g.wait_ge(T.sem.ld_stage, 16)
    sent = 0
    if relays:
        sent += _write(g, T, topo, core, [k for k, _ in relays], T.stage[:, :], T.stage[:, :], T.sem.handed,
                       _hand_mask(topo, cores, rank, plan))
    if direct:
        dsts = [cores[j] for j in direct]
        sent += _write(g, T, topo, core, dsts, T.stage[:, :], own, T.sem["arr%d" % rank],
                       _common_mask(topo, core, dsts))

    expect = []
    for i, (d_i, r_i) in enumerate(plan):
        if rank in d_i:
            m = _common_mask(topo, cores[i], [cores[j] for j in d_i])
            expect.append(((0, d_i.index(rank), 0), i, _count(m)))
        for pos, (k, ranks) in enumerate(r_i):
            if rank in ranks:
                m = _common_mask(topo, k, [cores[j] for j in ranks])
                expect.append(((1, ranks.index(rank), pos), i, _count(m)))
    expect.sort()
    jobs = [[e] for e in expect]
    while len(jobs) > BANKS:
        jobs = [jobs[0] + jobs[1]] + jobs[2:]

    g.tensor.wait_ge(T.sem.ld_land, 16)
    for b, job in enumerate(jobs):
        for n_in_job, (_, s, inc) in enumerate(job):
            g.tensor.wait_ge(T.sem["arr%d" % s], inc)
            out = T["ps%d" % b][0:C, n_in_job * C:(n_in_job + 1) * C]
            for t in range(KT):
                mm = g.tensor.matmul(out, T.land[:, rank * W + t * C:rank * W + (t + 1) * C],
                                     T.land[:, s * W + t * C:s * W + (t + 1) * C], t == 0, t == KT - 1)
            mm.then_inc(T.sem["mm%d" % b], 1)

    for b, job in enumerate(jobs):
        g.vector.wait_ge(T.sem["mm%d" % b], len(job))
        for n_in_job, (_, s, inc) in enumerate(job):
            g.vector.tensor_copy(T.ysb[0:C, s * C:(s + 1) * C],
                                 T["ps%d" % b][0:C, n_in_job * C:(n_in_job + 1) * C]).then_inc(T.sem["cp%d" % b], 1)

    queues = [g.sync, g.scalar]
    stored = [0, 0]
    for b, job in enumerate(jobs):
        w = b % 2
        queues[w].wait_ge(T.sem["cp%d" % b], len(job))
        for _, s, inc in job:
            queues[w].dma_start(T.y[:, s * C:(s + 1) * C], T.ysb[0:C, s * C:(s + 1) * C]).then_inc(T.sem["st%d" % w], 16)
            stored[w] += 16
    for w in range(2):
        queues[w].wait_ge(T.sem["st%d" % w], stored[w])
    g.wait_ge(T.sem.sent, sent)
